import numpy as np, ml_dtypes
CORES = [16,32,48,64,80]
N = 5
NB, B = 8, 128
def setup_inputs(rng):
    return {"x": rng.standard_normal((N, 128, NB * B), dtype=np.float32).astype(ml_dtypes.bfloat16), "wv": (rng.standard_normal((N, 128, 128), dtype=np.float32) / 16).astype(ml_dtypes.bfloat16), "wh": (rng.standard_normal((N, 128, 128), dtype=np.float32) / 16).astype(ml_dtypes.bfloat16)}
def setup_inputs_big(rng):
    d = setup_inputs(rng)
    for k in ("x",): d[k] = (d[k].astype(np.float32) * 1048576.0).astype(d[k].dtype)
    return d
def setup_inputs_small(rng):
    d = setup_inputs(rng)
    for k in ("x",): d[k] = (d[k].astype(np.float32) * (1 / 1048576.0)).astype(d[k].dtype)
    return d
def setup_inputs_apart(rng):
    d = setup_inputs(rng)
    f = (10.0 ** rng.permutation(np.linspace(-1.5, 1.5, N))).astype(np.float32).reshape(N, 1, 1)
    for k in ("x",): d[k] = (d[k].astype(np.float32) * f).astype(d[k].dtype)
    return d
def reference(x, wv, wh):
    X, WV, WH = x.astype(np.float64), wv.astype(np.float64), wh.astype(np.float64)
    h = np.zeros((N, NB, 128, B))
    for r in range(N):
        for c in range(NB):
            a = X[r][:, B * c:B * c + B].copy()
            if r: a += WV[r].T @ h[r - 1][c]
            if c: a += WH[r].T @ h[r][c - 1]
            h[r][c] = np.maximum(a, 0.0)
    return {"y": np.concatenate([h[:, c] for c in range(NB)], axis=2).astype(ml_dtypes.bfloat16)}

@@ -1,0 +1,165 @@
+from concourse.mybir import dt, AluOpType
+
+NB, B = 8, 128
+MSGS = [(c, c + 1) for c in range(NB)]
+
+SCRATCH = {
+    "xs": ("sbuf", [128, NB * B], "bfloat16"),
+    "up": ("sbuf", [128, NB * B], "bfloat16"),
+    "hs": ("sbuf", [128, NB * B], "bfloat16"),
+    "qs": ("sbuf", [128, NB * B], "bfloat16"),
+    "wvs": ("sbuf", [128, B], "bfloat16"),
+    "whs": ("sbuf", [128, B], "bfloat16"),
+    "nwh": ("sbuf", [128, B], "bfloat16"),
+    "zer": ("sbuf", [128, B], "bfloat16"),
+    "zid": ("sbuf", [128, B + 1], "bfloat16"),
+    "ident": ("sbuf", [128, B], "bfloat16"),
+    "idd": ("dram", [B + 1, 128], "bfloat16"),
+}
+for _c in range(NB):
+    SCRATCH["ps%d" % _c] = ("psum", [128, 512], "float32")
+
+SEMAPHORES = (["arr%d" % j for j in range(NB)] + ["hv%d" % c for c in range(NB)] + ["qv%d" % c for c in range(NB)]
+              + ["mm%d" % c for c in range(NB)]
+              + ["ldx0", "ldx1", "ldx2", "ldwv", "ldwh", "fillz", "filli", "ida", "idb", "nw", "sent", "st"])
+
+
+def _bits(m):
+    return bin(m).count("1")
+
+
+def rank_program(g, core, T, topo):
+    rank = T.rank_of(core)
+    if rank is None:
+        return
+    n = len(T.cores)
+    first, last = rank == 0, rank == n - 1
+    S = T.sem
+    tot = {}
+    seen = set()
+
+    def inc(instr, name, k):
+        instr.then_inc(S[name], k)
+        tot[name] = tot.get(name, 0) + k
+
+    def need(qname, q, name, val):
+        if (qname, name, val) not in seen:
+            seen.add((qname, name, val))
+            q.wait_ge(S[name], val)
+
+    def cols(a, b=None):
+        return slice(a * B, (a + 1 if b is None else b) * B)
+
+    te, ve, sy, sc = g.tensor, g.vector, g.sync, g.scalar
+    ps = [T["ps%d" % c][:, 0:B] for c in range(NB)]
+    msg_of = {}
+    for j, (a, b) in enumerate(MSGS):
+        for c in range(a, b):
+            msg_of[c] = j
+
+    if first:
+        xsem = ["ldx0"] + ["ldx1"] * 3 + ["ldx2"] * 4
+        inc(sy.dma_start(T.xs[:, cols(0)], T.x[:, cols(0)]), "ldx0", 16)
+        inc(sc.dma_start(T.whs[:], T.wh[:]), "ldwh", 16)
+        inc(sy.dma_start(T.xs[:, cols(1, 4)], T.x[:, cols(1, 4)]), "ldx1", 16)
+        inc(sc.dma_start(T.xs[:, cols(4, 8)], T.x[:, cols(4, 8)]), "ldx2", 16)
+        inc(ve.memset(T.zer[:], 0.0), "fillz", 1)
+    else:
+        xsem = ["ldx0"] * NB
+        inc(ve.memset(T.zid[:, 0:B], 0.0), "filli", 1)
+        inc(ve.memset(T.zid[:, B:B + 1], 1.0), "filli", 1)
+        inc(ve.memset(T.zer[:], 0.0), "fillz", 1)
+        inc(sc.dma_start(T.xs[:], T.x[:]), "ldx0", 16)
+        inc(sc.dma_start(T.wvs[:], T.wv[:]), "ldwv", 16)
+        inc(sc.dma_start(T.whs[:], T.wh[:]), "ldwh", 16)
+        need("sy", sy, "filli", 2)
+        inc(sy.dma_start(T.idd[:], T.zid[:]), "ida", 16)
+        need("sy", sy, "ida", 16)
+        inc(sy.dma_start(T.ident[:], T.idd[1:B + 1, :]), "idb", 16)
+        src = T.cores[rank - 1]
+        for j in range(len(MSGS)):
+            tot["arr%d" % j] = _bits(topo.mask(src, core))
+
+    need("ve", ve, "fillz", 1)
+    if first:
+        need("ve", ve, "ldx0", 16)
+        inc(ve.tensor_tensor(T.hs[:, cols(0)], T.xs[:, cols(0)], T.zer[:], op=AluOpType.max), "hv0", 1)
+        need("ve", ve, "ldwh", 16)
+        inc(ve.tensor_tensor(T.nwh[:], T.zer[:], T.whs[:], op=AluOpType.subtract), "nw", 1)
+        need("te", te, "nw", 1)
+        need("te", te, "ldwh", 16)
+        need("te", te, "hv0", 1)
+        inc(te.matmul(ps[1], T.nwh[:], T.hs[:, cols(0)], start=True, stop=True), "mm1", 1)
+        pre = [2]
+
+        def preload(upto):
+            while pre[0] <= min(upto, NB - 1):
+                c = pre[0]
+                need("te", te, xsem[c - 1], 16)
+                inc(te.matmul(ps[c], T.nwh[:], T.xs[:, cols(c - 1)], start=True, stop=False), "mm%d" % c, 1)
+                pre[0] += 1
+
+        preload(3)
+        for c in range(1, NB):
+            if c > 1:
+                need("te", te, "qv%d" % (c - 1), 1)
+                inc(te.matmul(ps[c], T.whs[:], T.qs[:, cols(c - 1)], start=False, stop=True), "mm%d" % c, 1)
+                preload(c + 2)
+            need("ve", ve, xsem[c], 16)
+            need("ve", ve, "mm%d" % c, tot["mm%d" % c])
+            inc(ve.tensor_tensor(T.qs[:, cols(c)], ps[c], T.xs[:, cols(c)], op=AluOpType.min), "qv%d" % c, 1)
+            need("ve", ve, "qv%d" % c, 1)
+            inc(ve.tensor_tensor(T.hs[:, cols(c)], T.xs[:, cols(c)], T.qs[:, cols(c)], op=AluOpType.subtract),
+                "hv%d" % c, 1)
+    else:
+        need("te", te, "idb", 16)
+        need("te", te, "ldx0", 16)
+        pre = [0]
+
+        def preload(upto):
+            while pre[0] <= min(upto, NB - 1):
+                c = pre[0]
+                inc(te.matmul(ps[c], T.ident[:], T.xs[:, cols(c)], start=True, stop=False), "mm%d" % c, 1)
+                pre[0] += 1
+
+        preload(1)
+        need("te", te, "ldwv", 16)
+        need("te", te, "ldwh", 16)
+        for c in range(NB):
+            j = msg_of[c]
+            if MSGS[j][0] == c:
+                preload(MSGS[j][1] - 1)
+                need("te", te, "arr%d" % j, tot["arr%d" % j])
+                for d in range(*MSGS[j]):
+                    inc(te.matmul(ps[d], T.wvs[:], T.up[:, cols(d)], start=False, stop=(d == 0)), "mm%d" % d, 1)
+            if c > 0:
+                need("te", te, "hv%d" % (c - 1), 1)
+                inc(te.matmul(ps[c], T.whs[:], T.hs[:, cols(c - 1)], start=False, stop=True), "mm%d" % c, 1)
+            preload(c + 2)
+            need("ve", ve, "mm%d" % c, tot["mm%d" % c])
+            inc(ve.tensor_tensor(T.hs[:, cols(c)], ps[c], T.zer[:], op=AluOpType.max), "hv%d" % c, 1)
+
+    if not last:
+        dst = T.cores[rank + 1]
+        rid, pid, _se = topo.addr(dst)
+        mask = topo.mask(core, dst)
+        for j, (a, b) in enumerate(MSGS):
+            for c in range(a, b):
+                need("g", g, "hv%d" % c, 1)
+            g.remote_dma(out_ap=T.up[:, cols(a, b)], in_ap=T.hs[:, cols(a, b)], remote_sem=S["arr%d" % j],
+                         local_sem=S.sent, pid=pid, routing_id=rid, dma_engine_mask=mask)
+            tot["sent"] = tot.get("sent", 0) + _bits(mask)
+        half = NB // 2
+        for qname, q, a, b in (("sy", sy, 0, half), ("sc", sc, half, NB)):
+            need(qname, q, "sent", tot["sent"])
+            for c in range(a, b):
+                need(qname, q, "hv%d" % c, 1)
+            inc(q.dma_start(T.y[:, cols(a, b)], T.hs[:, cols(a, b)]), "st", 16)
+    else:
+        for c in range(NB):
+            qname, q = (("sy", sy), ("sc", sc))[c % 2]
+            need(qname, q, "hv%d" % c, 1)
+            inc(q.dma_start(T.y[:, cols(c)], T.hs[:, cols(c)]), "st", 16)
+
+    for name in sorted(tot):
+        need("g", g, name, tot[name])

@@ -1,15 +1,17 @@
 from concourse.mybir import dt, AluOpType
 
 NB, B = 8, 128
-MSGS = [(c, c + 1) for c in range(NB)]
+NW = 2
+PIECES = [(0, 2), (2, 5), (5, 8)]
+RELAYED = 2
 
 SCRATCH = {
-    "xs": ("sbuf", [128, NB * B], "bfloat16"),
+    "pk": ("sbuf", [128, (NB + NW) * B], "bfloat16"),
+    "upk": ("sbuf", [128, (NB + NW) * B], "bfloat16"),
     "up": ("sbuf", [128, NB * B], "bfloat16"),
+    "ha": ("sbuf", [128, NB * B], "bfloat16"),
     "hs": ("sbuf", [128, NB * B], "bfloat16"),
     "qs": ("sbuf", [128, NB * B], "bfloat16"),
-    "wvs": ("sbuf", [128, B], "bfloat16"),
-    "whs": ("sbuf", [128, B], "bfloat16"),
     "nwh": ("sbuf", [128, B], "bfloat16"),
     "zer": ("sbuf", [128, B], "bfloat16"),
     "zid": ("sbuf", [128, B + 1], "bfloat16"),
@@ -19,22 +21,48 @@ SCRATCH = {
 for _c in range(NB):
     SCRATCH["ps%d" % _c] = ("psum", [128, 512], "float32")
 
-SEMAPHORES = (["arr%d" % j for j in range(NB)] + ["hv%d" % c for c in range(NB)] + ["qv%d" % c for c in range(NB)]
-              + ["mm%d" % c for c in range(NB)]
-              + ["ldx0", "ldx1", "ldx2", "ldwv", "ldwh", "fillz", "filli", "ida", "idb", "nw", "sent", "st"])
+SEMAPHORES = ([p + str(c) for p in ("arr", "hv", "hu", "qv", "mm", "ma") for c in range(NB)]
+              + ["bk0", "bk1", "bk2", "ldx0", "ldx1", "ldx2", "ldwv", "ldwh",
+                 "fillz", "filli", "ida", "idb", "nw", "sent", "st"])
 
 
 def _bits(m):
     return bin(m).count("1")
 
 
+def _cols(a, b=None):
+    return slice(a * B, (a + 1 if b is None else b) * B)
+
+
+def _relay_of(c0, T, topo):
+    for c in range(topo.CHIPS * topo.CORES_PER_CHIP):
+        if topo.chip(c) == topo.chip(c0) and topo.die(c) != topo.die(c0) and T.rank_of(c) is None:
+            return c
+    return None
+
+
 def rank_program(g, core, T, topo):
     rank = T.rank_of(core)
-    if rank is None:
-        return
     n = len(T.cores)
-    first, last = rank == 0, rank == n - 1
     S = T.sem
+    cols = _cols
+    ra, rb = PIECES[RELAYED]
+    rcols = cols(ra + NW, rb + NW)
+    rsem = "bk%d" % RELAYED
+
+    if rank is None:
+        for r in range(n - 1):
+            src, dst = T.cores[r], T.cores[r + 1]
+            if _relay_of(src, T, topo) == core:
+                on_chip = topo.mask(src, core) & ~topo.mask(src, dst)
+                g.wait_ge(S[rsem], _bits(on_chip))
+                rid, pid, _se = topo.addr(dst)
+                mask = topo.mask(core, dst)
+                g.remote_dma(out_ap=T.upk[:, rcols], in_ap=T.upk[:, rcols], remote_sem=S[rsem], local_sem=S.sent,
+                             pid=pid, routing_id=rid, dma_engine_mask=mask)
+                g.wait_ge(S.sent, _bits(mask))
+        return
+
     tot = {}
     seen = set()
 
@@ -42,124 +70,191 @@ def rank_program(g, core, T, topo):
         instr.then_inc(S[name], k)
         tot[name] = tot.get(name, 0) + k
 
-    def need(qname, q, name, val):
+    def need(qname, q, name, val=None):
+        val = tot[name] if val is None else val
         if (qname, name, val) not in seen:
             seen.add((qname, name, val))
             q.wait_ge(S[name], val)
 
-    def cols(a, b=None):
-        return slice(a * B, (a + 1 if b is None else b) * B)
+    def xc(c, d=None):
+        return cols(c + NW, None if d is None else d + NW)
 
     te, ve, sy, sc = g.tensor, g.vector, g.sync, g.scalar
     ps = [T["ps%d" % c][:, 0:B] for c in range(NB)]
-    msg_of = {}
-    for j, (a, b) in enumerate(MSGS):
+    piece = {}
+    for j, (a, b) in enumerate(PIECES):
         for c in range(a, b):
-            msg_of[c] = j
+            piece[c] = j
+    WV, WH = cols(0), cols(1)
+    has_a = rank >= 1
+    has_up = rank >= 2
+    sends_in = rank + 1 < n
+    sends_h = rank + 2 < n
 
-    if first:
-        xsem = ["ldx0"] + ["ldx1"] * 3 + ["ldx2"] * 4
-        inc(sy.dma_start(T.xs[:, cols(0)], T.x[:, cols(0)]), "ldx0", 16)
-        inc(sc.dma_start(T.whs[:], T.wh[:]), "ldwh", 16)
-        inc(sy.dma_start(T.xs[:, cols(1, 4)], T.x[:, cols(1, 4)]), "ldx1", 16)
-        inc(sc.dma_start(T.xs[:, cols(4, 8)], T.x[:, cols(4, 8)]), "ldx2", 16)
-        inc(ve.memset(T.zer[:], 0.0), "fillz", 1)
-    else:
-        xsem = ["ldx0"] * NB
+    def load_x(q, j):
+        a, b = PIECES[j]
+        inc(q.dma_start(T.pk[:, xc(a, b)], T.x[:, cols(a, b)]), "ldx%d" % j, 16)
+
+    load_x(sy, 0)
+    inc(sc.dma_start(T.pk[:, WH], T.wh[:]), "ldwh", 16)
+    if has_a:
+        inc(sc.dma_start(T.pk[:, WV], T.wv[:]), "ldwv", 16)
         inc(ve.memset(T.zid[:, 0:B], 0.0), "filli", 1)
         inc(ve.memset(T.zid[:, B:B + 1], 1.0), "filli", 1)
-        inc(ve.memset(T.zer[:], 0.0), "fillz", 1)
-        inc(sc.dma_start(T.xs[:], T.x[:]), "ldx0", 16)
-        inc(sc.dma_start(T.wvs[:], T.wv[:]), "ldwv", 16)
-        inc(sc.dma_start(T.whs[:], T.wh[:]), "ldwh", 16)
-        need("sy", sy, "filli", 2)
+        load_x(sc, 2)
+        load_x(sc, 1)
+        need("sy", sy, "filli")
         inc(sy.dma_start(T.idd[:], T.zid[:]), "ida", 16)
-        need("sy", sy, "ida", 16)
+        need("sy", sy, "ida")
         inc(sy.dma_start(T.ident[:], T.idd[1:B + 1, :]), "idb", 16)
-        src = T.cores[rank - 1]
-        for j in range(len(MSGS)):
-            tot["arr%d" % j] = _bits(topo.mask(src, core))
+        prev = T.cores[rank - 1]
+        for j in range(len(PIECES)):
+            tot["bk%d" % j] = _bits(topo.mask(_relay_of(prev, T, topo) if j == RELAYED else prev, core))
+    else:
+        load_x(sc, 2)
+        load_x(sy, 1)
+    if has_up:
+        for c in range(NB):
+            tot["arr%d" % c] = _bits(topo.mask(T.cores[rank - 2], core))
+    inc(ve.memset(T.zer[:], 0.0), "fillz", 1)
 
-    need("ve", ve, "fillz", 1)
-    if first:
-        need("ve", ve, "ldx0", 16)
-        inc(ve.tensor_tensor(T.hs[:, cols(0)], T.xs[:, cols(0)], T.zer[:], op=AluOpType.max), "hv0", 1)
-        need("ve", ve, "ldwh", 16)
-        inc(ve.tensor_tensor(T.nwh[:], T.zer[:], T.whs[:], op=AluOpType.subtract), "nw", 1)
-        need("te", te, "nw", 1)
-        need("te", te, "ldwh", 16)
-        need("te", te, "hv0", 1)
+    need("ve", ve, "fillz")
+    if not has_a:
+        need("ve", ve, "ldx0")
+        inc(ve.tensor_tensor(T.hs[:, cols(0)], T.pk[:, xc(0)], T.zer[:], op=AluOpType.max), "hv0", 1)
+        need("ve", ve, "ldwh")
+        inc(ve.tensor_tensor(T.nwh[:], T.zer[:], T.pk[:, WH], op=AluOpType.subtract), "nw", 1)
+        need("te", te, "nw")
+        need("te", te, "ldwh")
+        need("te", te, "hv0")
         inc(te.matmul(ps[1], T.nwh[:], T.hs[:, cols(0)], start=True, stop=True), "mm1", 1)
         pre = [2]
 
         def preload(upto):
             while pre[0] <= min(upto, NB - 1):
                 c = pre[0]
-                need("te", te, xsem[c - 1], 16)
-                inc(te.matmul(ps[c], T.nwh[:], T.xs[:, cols(c - 1)], start=True, stop=False), "mm%d" % c, 1)
+                need("te", te, "ldx%d" % piece[c - 1])
+                inc(te.matmul(ps[c], T.nwh[:], T.pk[:, xc(c - 1)], start=True, stop=False), "mm%d" % c, 1)
                 pre[0] += 1
 
-        preload(3)
+        preload(2)
         for c in range(1, NB):
             if c > 1:
-                need("te", te, "qv%d" % (c - 1), 1)
-                inc(te.matmul(ps[c], T.whs[:], T.qs[:, cols(c - 1)], start=False, stop=True), "mm%d" % c, 1)
-                preload(c + 2)
-            need("ve", ve, xsem[c], 16)
-            need("ve", ve, "mm%d" % c, tot["mm%d" % c])
-            inc(ve.tensor_tensor(T.qs[:, cols(c)], ps[c], T.xs[:, cols(c)], op=AluOpType.min), "qv%d" % c, 1)
-            need("ve", ve, "qv%d" % c, 1)
-            inc(ve.tensor_tensor(T.hs[:, cols(c)], T.xs[:, cols(c)], T.qs[:, cols(c)], op=AluOpType.subtract),
+                need("te", te, "qv%d" % (c - 1))
+                inc(te.matmul(ps[c], T.pk[:, WH], T.qs[:, cols(c - 1)], start=False, stop=True), "mm%d" % c, 1)
+            preload(c + 2)
+            need("ve", ve, "ldx%d" % piece[c])
+            need("ve", ve, "mm%d" % c)
+            inc(ve.tensor_tensor(T.qs[:, cols(c)], ps[c], T.pk[:, xc(c)], op=AluOpType.min), "qv%d" % c, 1)
+            need("ve", ve, "qv%d" % c)
+            inc(ve.tensor_tensor(T.hs[:, cols(c)], T.pk[:, xc(c)], T.qs[:, cols(c)], op=AluOpType.subtract),
                 "hv%d" % c, 1)
     else:
-        need("te", te, "idb", 16)
-        need("te", te, "ldx0", 16)
-        pre = [0]
+        nbk = NB // 2
+        psa = [ps[c % nbk] for c in range(NB)]
+        psb = [ps[nbk + c % nbk] for c in range(NB)]
+        pa, pb = [0], [0]
+        ahead = nbk - 1 if rank >= 3 else 1
 
-        def preload(upto):
-            while pre[0] <= min(upto, NB - 1):
-                c = pre[0]
-                inc(te.matmul(ps[c], T.ident[:], T.xs[:, cols(c)], start=True, stop=False), "mm%d" % c, 1)
-                pre[0] += 1
+        def preload_a(upto):
+            while pa[0] <= min(upto, NB - 1):
+                c = pa[0]
+                need("te", te, "bk%d" % piece[c])
+                if c >= nbk:
+                    need("te", te, "hu%d" % (c - nbk))
+                inc(te.matmul(psa[c], T.ident[:], T.upk[:, xc(c)], start=True, stop=(c == 0 and not has_up)),
+                    "ma%d" % c, 1)
+                pa[0] += 1
 
-        preload(1)
-        need("te", te, "ldwv", 16)
-        need("te", te, "ldwh", 16)
-        for c in range(NB):
-            j = msg_of[c]
-            if MSGS[j][0] == c:
-                preload(MSGS[j][1] - 1)
-                need("te", te, "arr%d" % j, tot["arr%d" % j])
-                for d in range(*MSGS[j]):
-                    inc(te.matmul(ps[d], T.wvs[:], T.up[:, cols(d)], start=False, stop=(d == 0)), "mm%d" % d, 1)
-            if c > 0:
-                need("te", te, "hv%d" % (c - 1), 1)
-                inc(te.matmul(ps[c], T.whs[:], T.hs[:, cols(c - 1)], start=False, stop=True), "mm%d" % c, 1)
-            preload(c + 2)
-            need("ve", ve, "mm%d" % c, tot["mm%d" % c])
-            inc(ve.tensor_tensor(T.hs[:, cols(c)], ps[c], T.zer[:], op=AluOpType.max), "hv%d" % c, 1)
+        def preload_b(upto):
+            while pb[0] <= min(upto, NB - 1):
+                c = pb[0]
+                need("te", te, "ldx%d" % piece[c])
+                if c >= nbk:
+                    need("te", te, "hv%d" % (c - nbk))
+                inc(te.matmul(psb[c], T.ident[:], T.pk[:, xc(c)], start=True, stop=False), "mm%d" % c, 1)
+                pb[0] += 1
 
-    if not last:
-        dst = T.cores[rank + 1]
+        need("te", te, "idb")
+        preload_b(nbk - 1)
+        need("te", te, "ldwv")
+        need("te", te, "ldwh")
+        preload_a(ahead - 1)
+        for t in range(NB + 1):
+            if t < NB:
+                if has_up:
+                    need("te", te, "arr%d" % t)
+                    inc(te.matmul(psa[t], T.upk[:, WV], T.up[:, cols(t)], start=False, stop=(t == 0)), "ma%d" % t, 1)
+                if t > 0:
+                    need("te", te, "hu%d" % (t - 1))
+                    inc(te.matmul(psa[t], T.upk[:, WH], T.ha[:, cols(t - 1)], start=False, stop=True), "ma%d" % t, 1)
+            if t > 0:
+                c = t - 1
+                need("te", te, "hu%d" % c)
+                inc(te.matmul(psb[c], T.pk[:, WV], T.ha[:, cols(c)], start=False, stop=(c == 0)), "mm%d" % c, 1)
+                if c > 0:
+                    need("te", te, "hv%d" % (c - 1))
+                    inc(te.matmul(psb[c], T.pk[:, WH], T.hs[:, cols(c - 1)], start=False, stop=True), "mm%d" % c, 1)
+            if t < NB:
+                need("ve", ve, "ma%d" % t)
+                inc(ve.tensor_tensor(T.ha[:, cols(t)], psa[t], T.zer[:], op=AluOpType.max), "hu%d" % t, 1)
+            if t > 0:
+                need("ve", ve, "mm%d" % (t - 1))
+                inc(ve.tensor_tensor(T.hs[:, cols(t - 1)], psb[t - 1], T.zer[:], op=AluOpType.max),
+                    "hv%d" % (t - 1), 1)
+            preload_a(t + ahead)
+            preload_b(t + 2)
+
+    def send(dst, out_ap, in_ap, sem, mask):
         rid, pid, _se = topo.addr(dst)
-        mask = topo.mask(core, dst)
-        for j, (a, b) in enumerate(MSGS):
-            for c in range(a, b):
-                need("g", g, "hv%d" % c, 1)
-            g.remote_dma(out_ap=T.up[:, cols(a, b)], in_ap=T.hs[:, cols(a, b)], remote_sem=S["arr%d" % j],
-                         local_sem=S.sent, pid=pid, routing_id=rid, dma_engine_mask=mask)
-            tot["sent"] = tot.get("sent", 0) + _bits(mask)
+        g.remote_dma(out_ap=out_ap, in_ap=in_ap, remote_sem=S[sem], local_sem=S.sent, pid=pid, routing_id=rid,
+                     dma_engine_mask=mask)
+        tot["sent"] = tot.get("sent", 0) + _bits(mask)
+
+    def send_in(j):
+        a, b = PIECES[j]
+        dst = T.cores[rank + 1]
+        need("g", g, "ldx%d" % j)
+        if j == RELAYED:
+            relay = _relay_of(core, T, topo)
+            send(relay, T.upk[:, rcols], T.pk[:, rcols], rsem, topo.mask(core, relay) & ~topo.mask(core, dst))
+            return
+        lo = a + NW
+        if j == 0:
+            need("g", g, "ldwh")
+            lo = 1
+            if has_a:
+                need("g", g, "ldwv")
+                lo = 0
+        send(dst, T.upk[:, cols(lo, b + NW)], T.pk[:, cols(lo, b + NW)], "bk%d" % j, topo.mask(core, dst))
+
+    def send_h(c):
+        dst = T.cores[rank + 2]
+        need("g", g, "hv%d" % c)
+        send(dst, T.up[:, cols(c)], T.hs[:, cols(c)], "arr%d" % c, topo.mask(core, dst))
+
+    if not has_a:
+        plan = ["h0", "i0", "i2", "h1", "i1", "h2", "h3", "h4", "h5", "h6", "h7"]
+    else:
+        plan = (["i0", "i2", "i1"] if sends_in else []) + (["h%d" % c for c in range(NB)] if sends_h else [])
+    for p in plan:
+        if p[0] == "i":
+            send_in(int(p[1:]))
+        else:
+            send_h(int(p[1:]))
+
+    if sends_h:
         half = NB // 2
         for qname, q, a, b in (("sy", sy, 0, half), ("sc", sc, half, NB)):
-            need(qname, q, "sent", tot["sent"])
+            need(qname, q, "sent")
             for c in range(a, b):
-                need(qname, q, "hv%d" % c, 1)
+                need(qname, q, "hv%d" % c)
             inc(q.dma_start(T.y[:, cols(a, b)], T.hs[:, cols(a, b)]), "st", 16)
     else:
         for c in range(NB):
             qname, q = (("sy", sy), ("sc", sc))[c % 2]
-            need(qname, q, "hv%d" % c, 1)
+            need(qname, q, "hv%d" % c)
             inc(q.dma_start(T.y[:, cols(c)], T.hs[:, cols(c)]), "st", 16)
 
     for name in sorted(tot):
-        need("g", g, name, tot[name])
+        need("g", g, name)

from concourse.mybir import dt, AluOpType

NB, B = 8, 128
NW = 2
PIECES = [(0, 2), (2, 5), (5, 8)]
RELAYED = 2

SCRATCH = {
    "pk": ("sbuf", [128, (NB + NW) * B], "bfloat16"),
    "upk": ("sbuf", [128, (NB + NW) * B], "bfloat16"),
    "up": ("sbuf", [128, NB * B], "bfloat16"),
    "ha": ("sbuf", [128, NB * B], "bfloat16"),
    "hs": ("sbuf", [128, NB * B], "bfloat16"),
    "qs": ("sbuf", [128, NB * B], "bfloat16"),
    "nwh": ("sbuf", [128, B], "bfloat16"),
    "zer": ("sbuf", [128, B], "bfloat16"),
    "zid": ("sbuf", [128, B + 1], "bfloat16"),
    "ident": ("sbuf", [128, B], "bfloat16"),
    "idd": ("dram", [B + 1, 128], "bfloat16"),
}
for _c in range(NB):
    SCRATCH["ps%d" % _c] = ("psum", [128, 512], "float32")

SEMAPHORES = ([p + str(c) for p in ("arr", "hv", "hu", "qv", "mm", "ma") for c in range(NB)]
              + ["bk0", "bk1", "bk2", "ldx0", "ldx1", "ldx2", "ldwv", "ldwh",
                 "fillz", "filli", "ida", "idb", "nw", "sent", "st"])


def _bits(m):
    return bin(m).count("1")


def _cols(a, b=None):
    return slice(a * B, (a + 1 if b is None else b) * B)


def _relay_of(c0, T, topo):
    for c in range(topo.CHIPS * topo.CORES_PER_CHIP):
        if topo.chip(c) == topo.chip(c0) and topo.die(c) != topo.die(c0) and T.rank_of(c) is None:
            return c
    return None


def rank_program(g, core, T, topo):
    rank = T.rank_of(core)
    n = len(T.cores)
    S = T.sem
    cols = _cols
    ra, rb = PIECES[RELAYED]
    rcols = cols(ra + NW, rb + NW)
    rsem = "bk%d" % RELAYED

    if rank is None:
        for r in range(n - 1):
            src, dst = T.cores[r], T.cores[r + 1]
            if _relay_of(src, T, topo) == core:
                on_chip = topo.mask(src, core) & ~topo.mask(src, dst)
                g.wait_ge(S[rsem], _bits(on_chip))
                rid, pid, _se = topo.addr(dst)
                mask = topo.mask(core, dst)
                g.remote_dma(out_ap=T.upk[:, rcols], in_ap=T.upk[:, rcols], remote_sem=S[rsem], local_sem=S.sent,
                             pid=pid, routing_id=rid, dma_engine_mask=mask)
                g.wait_ge(S.sent, _bits(mask))
        return

    tot = {}
    seen = set()

    def inc(instr, name, k):
        instr.then_inc(S[name], k)
        tot[name] = tot.get(name, 0) + k

    def need(qname, q, name, val=None):
        val = tot[name] if val is None else val
        if (qname, name, val) not in seen:
            seen.add((qname, name, val))
            q.wait_ge(S[name], val)

    def xc(c, d=None):
        return cols(c + NW, None if d is None else d + NW)

    te, ve, sy, sc = g.tensor, g.vector, g.sync, g.scalar
    ps = [T["ps%d" % c][:, 0:B] for c in range(NB)]
    piece = {}
    for j, (a, b) in enumerate(PIECES):
        for c in range(a, b):
            piece[c] = j
    WV, WH = cols(0), cols(1)
    has_a = rank >= 1
    has_up = rank >= 2
    sends_in = rank + 1 < n
    sends_h = rank + 2 < n

    def load_x(q, j):
        a, b = PIECES[j]
        inc(q.dma_start(T.pk[:, xc(a, b)], T.x[:, cols(a, b)]), "ldx%d" % j, 16)

    load_x(sy, 0)
    inc(sc.dma_start(T.pk[:, WH], T.wh[:]), "ldwh", 16)
    if has_a:
        inc(sc.dma_start(T.pk[:, WV], T.wv[:]), "ldwv", 16)
        inc(ve.memset(T.zid[:, 0:B], 0.0), "filli", 1)
        inc(ve.memset(T.zid[:, B:B + 1], 1.0), "filli", 1)
        load_x(sc, 2)
        load_x(sc, 1)
        need("sy", sy, "filli")
        inc(sy.dma_start(T.idd[:], T.zid[:]), "ida", 16)
        need("sy", sy, "ida")
        inc(sy.dma_start(T.ident[:], T.idd[1:B + 1, :]), "idb", 16)
        prev = T.cores[rank - 1]
        for j in range(len(PIECES)):
            tot["bk%d" % j] = _bits(topo.mask(_relay_of(prev, T, topo) if j == RELAYED else prev, core))
    else:
        load_x(sc, 2)
        load_x(sy, 1)
    if has_up:
        for c in range(NB):
            tot["arr%d" % c] = _bits(topo.mask(T.cores[rank - 2], core))
    inc(ve.memset(T.zer[:], 0.0), "fillz", 1)

    need("ve", ve, "fillz")
    if not has_a:
        need("ve", ve, "ldx0")
        inc(ve.tensor_tensor(T.hs[:, cols(0)], T.pk[:, xc(0)], T.zer[:], op=AluOpType.max), "hv0", 1)
        need("ve", ve, "ldwh")
        inc(ve.tensor_tensor(T.nwh[:], T.zer[:], T.pk[:, WH], op=AluOpType.subtract), "nw", 1)
        need("te", te, "nw")
        need("te", te, "ldwh")
        need("te", te, "hv0")
        inc(te.matmul(ps[1], T.nwh[:], T.hs[:, cols(0)], start=True, stop=True), "mm1", 1)
        pre = [2]

        def preload(upto):
            while pre[0] <= min(upto, NB - 1):
                c = pre[0]
                need("te", te, "ldx%d" % piece[c - 1])
                inc(te.matmul(ps[c], T.nwh[:], T.pk[:, xc(c - 1)], start=True, stop=False), "mm%d" % c, 1)
                pre[0] += 1

        preload(2)
        for c in range(1, NB):
            if c > 1:
                need("te", te, "qv%d" % (c - 1))
                inc(te.matmul(ps[c], T.pk[:, WH], T.qs[:, cols(c - 1)], start=False, stop=True), "mm%d" % c, 1)
            preload(c + 2)
            need("ve", ve, "ldx%d" % piece[c])
            need("ve", ve, "mm%d" % c)
            inc(ve.tensor_tensor(T.qs[:, cols(c)], ps[c], T.pk[:, xc(c)], op=AluOpType.min), "qv%d" % c, 1)
            need("ve", ve, "qv%d" % c)
            inc(ve.tensor_tensor(T.hs[:, cols(c)], T.pk[:, xc(c)], T.qs[:, cols(c)], op=AluOpType.subtract),
                "hv%d" % c, 1)
    else:
        nbk = NB // 2
        psa = [ps[c % nbk] for c in range(NB)]
        psb = [ps[nbk + c % nbk] for c in range(NB)]
        pa, pb = [0], [0]
        ahead = nbk - 1 if rank >= 3 else 1

        def preload_a(upto):
            while pa[0] <= min(upto, NB - 1):
                c = pa[0]
                need("te", te, "bk%d" % piece[c])
                if c >= nbk:
                    need("te", te, "hu%d" % (c - nbk))
                inc(te.matmul(psa[c], T.ident[:], T.upk[:, xc(c)], start=True, stop=(c == 0 and not has_up)),
                    "ma%d" % c, 1)
                pa[0] += 1

        def preload_b(upto):
            while pb[0] <= min(upto, NB - 1):
                c = pb[0]
                need("te", te, "ldx%d" % piece[c])
                if c >= nbk:
                    need("te", te, "hv%d" % (c - nbk))
                inc(te.matmul(psb[c], T.ident[:], T.pk[:, xc(c)], start=True, stop=False), "mm%d" % c, 1)
                pb[0] += 1

        need("te", te, "idb")
        preload_b(nbk - 1)
        need("te", te, "ldwv")
        need("te", te, "ldwh")
        preload_a(ahead - 1)
        for t in range(NB + 1):
            if t < NB:
                if has_up:
                    need("te", te, "arr%d" % t)
                    inc(te.matmul(psa[t], T.upk[:, WV], T.up[:, cols(t)], start=False, stop=(t == 0)), "ma%d" % t, 1)
                if t > 0:
                    need("te", te, "hu%d" % (t - 1))
                    inc(te.matmul(psa[t], T.upk[:, WH], T.ha[:, cols(t - 1)], start=False, stop=True), "ma%d" % t, 1)
            if t > 0:
                c = t - 1
                need("te", te, "hu%d" % c)
                inc(te.matmul(psb[c], T.pk[:, WV], T.ha[:, cols(c)], start=False, stop=(c == 0)), "mm%d" % c, 1)
                if c > 0:
                    need("te", te, "hv%d" % (c - 1))
                    inc(te.matmul(psb[c], T.pk[:, WH], T.hs[:, cols(c - 1)], start=False, stop=True), "mm%d" % c, 1)
            if t < NB:
                need("ve", ve, "ma%d" % t)
                inc(ve.tensor_tensor(T.ha[:, cols(t)], psa[t], T.zer[:], op=AluOpType.max), "hu%d" % t, 1)
            if t > 0:
                need("ve", ve, "mm%d" % (t - 1))
                inc(ve.tensor_tensor(T.hs[:, cols(t - 1)], psb[t - 1], T.zer[:], op=AluOpType.max),
                    "hv%d" % (t - 1), 1)
            preload_a(t + ahead)
            preload_b(t + 2)

    def send(dst, out_ap, in_ap, sem, mask):
        rid, pid, _se = topo.addr(dst)
        g.remote_dma(out_ap=out_ap, in_ap=in_ap, remote_sem=S[sem], local_sem=S.sent, pid=pid, routing_id=rid,
                     dma_engine_mask=mask)
        tot["sent"] = tot.get("sent", 0) + _bits(mask)

    def send_in(j):
        a, b = PIECES[j]
        dst = T.cores[rank + 1]
        need("g", g, "ldx%d" % j)
        if j == RELAYED:
            relay = _relay_of(core, T, topo)
            send(relay, T.upk[:, rcols], T.pk[:, rcols], rsem, topo.mask(core, relay) & ~topo.mask(core, dst))
            return
        lo = a + NW
        if j == 0:
            need("g", g, "ldwh")
            lo = 1
            if has_a:
                need("g", g, "ldwv")
                lo = 0
        send(dst, T.upk[:, cols(lo, b + NW)], T.pk[:, cols(lo, b + NW)], "bk%d" % j, topo.mask(core, dst))

    def send_h(c):
        dst = T.cores[rank + 2]
        need("g", g, "hv%d" % c)
        send(dst, T.up[:, cols(c)], T.hs[:, cols(c)], "arr%d" % c, topo.mask(core, dst))

    if not has_a:
        plan = ["h0", "i0", "i2", "h1", "i1", "h2", "h3", "h4", "h5", "h6", "h7"]
    else:
        plan = (["i0", "i2", "i1"] if sends_in else []) + (["h%d" % c for c in range(NB)] if sends_h else [])
    for p in plan:
        if p[0] == "i":
            send_in(int(p[1:]))
        else:
            send_h(int(p[1:]))

    if sends_h:
        half = NB // 2
        for qname, q, a, b in (("sy", sy, 0, half), ("sc", sc, half, NB)):
            need(qname, q, "sent")
            for c in range(a, b):
                need(qname, q, "hv%d" % c)
            inc(q.dma_start(T.y[:, cols(a, b)], T.hs[:, cols(a, b)]), "st", 16)
    else:
        for c in range(NB):
            qname, q = (("sy", sy), ("sc", sc))[c % 2]
            need(qname, q, "hv%d" % c)
            inc(q.dma_start(T.y[:, cols(c)], T.hs[:, cols(c)]), "st", 16)

    for name in sorted(tot):
        need("g", g, name)
